import numpy as np
import ml_dtypes


def mxq(x, axis, fmt="e4m3"):
    dtype, down = {"e4m3": (ml_dtypes.float8_e4m3fn, 7), "e5m2": (ml_dtypes.float8_e5m2, 14)}[fmt]
    v = np.moveaxis(np.asarray(x, np.float32).astype(ml_dtypes.bfloat16).astype(np.float64), axis, -1)
    blocks = v.reshape(v.shape[:-1] + (-1, 32))
    amax = np.abs(blocks).max(-1, keepdims=True)
    byte = np.maximum(np.where(amax > 0, np.frexp(amax)[1] - 1 + 127, 0) - down, 1)
    scale = np.exp2(byte - 127.0)
    codes = (blocks / scale).astype(np.float32).astype(dtype).astype(np.float64)
    return np.moveaxis((codes * scale).reshape(v.shape), -1, axis)


WIDE = False


def mx_kscale(k):
    if not WIDE:
        return np.ones(k)
    levels = np.array([30, -30])
    if k % 512:
        return np.exp2(np.random.permutation(np.resize(levels, k // 32))).repeat(32)
    a = np.empty((k // 512, 16))
    for p in range(k // 512):
        a[p, :8] = np.random.permutation(np.resize(levels, 8))
        for g in range(8):
            far = levels[np.abs(levels - a[p, g]) >= 10]
            a[p, g + 8] = far[np.random.randint(len(far))]
    return np.exp2(a.ravel()).repeat(32)


def f64(x):
    return np.asarray(x).astype(np.float64)


K, L, M, T = 1536, 512, 1024, 512


def setup_inputs():
    n = np.random.standard_normal
    s1 = mx_kscale(K)[:, None]
    s2 = mx_kscale(L)[:, None]
    m = np.exp(0.5 * n((1, T)))
    return {
        "w": (n((K, M)) / np.sqrt(K) / s1).astype(np.float32),
        "dy": (m * n((K, T)) * s1).astype(np.float32),
        "v": (n((L, M)) / np.sqrt(L) / s2).astype(np.float32),
        "e": (n((L, T)) * s2).astype(np.float32),
        "r": (n((1024, 512))).astype(np.float32),
    }


def reference(w, dy, v, e, r):
    w_ = mxq(f64(w), 0, "e4m3")
    dy_ = mxq(f64(dy), 0, "e5m2")
    v_ = mxq(f64(v), 0, "e4m3")
    e_ = mxq(f64(e), 0, "e4m3")
    y = w_.T @ dy_ + v_.T @ e_
    return f64(r) + y

@@ -1,0 +1,134 @@
+from contextlib import ExitStack
+
+import concourse.mybir as mybir
+
+K, L, D, T = 1536, 512, 1024, 512
+
+FLOPS = 2 * (K + L) * D * T
+
+F32 = mybir.dt.float32
+BF16 = mybir.dt.bfloat16
+U32 = mybir.dt.uint32
+U8 = mybir.dt.uint8
+E4M3 = mybir.dt.float8_e4m3fn_x4
+E5M2 = mybir.dt.float8_e5m2_x4
+
+P = 128
+PACK = 4
+K_PASS = P * PACK
+GROUP = 512
+IN_GROUP = 4
+
+
+def tile_mix_aux_fm_res_kernel(tc, w, dy, v, e, r, out):
+    nc = tc.nc
+    banks = D // P
+    groups = D // GROUP
+
+    with ExitStack() as ctx:
+        keep = ctx.enter_context(tc.tile_pool(name="keep", bufs=1))
+        psum = ctx.enter_context(tc.psum_pool(name="psum", bufs=1))
+        ctx.enter_context(tc.manual_schedule())
+
+        def load(src, c, name):
+            width = src.shape[1]
+            raw = keep.tile([P, PACK, width], F32, name=name + "_raw", align_bytes=64)
+            rows = src[c * K_PASS:(c + 1) * K_PASS, :]
+            nc.sync.dma_start(out=raw[:], in_=rows.rearrange("(p j) c -> p j c", j=PACK))
+            return raw
+
+        dy_raw = {}
+        w_raw = {}
+        dy_raw[0] = load(dy, 0, "dy0")
+        w_raw[0] = load(w, 0, "w0")
+        dy_raw[1] = load(dy, 1, "dy1")
+        w_raw[1] = load(w, 1, "w1")
+        w_raw[2] = load(w, 2, "w2")
+        v_raw = load(v, 0, "v")
+        dy_raw[2] = load(dy, 2, "dy2")
+        e_raw = load(e, 0, "e")
+
+        r_sb = keep.tile([P, banks, T], F32, name="r_sb", align_bytes=64)
+        for g in range(groups):
+            rows = r[g * GROUP:(g + 1) * GROUP, :]
+            nc.sync.dma_start(
+                out=r_sb[:, g * IN_GROUP:(g + 1) * IN_GROUP, :],
+                in_=rows.rearrange("(m t) n -> m t n", t=IN_GROUP),
+            )
+
+        def stationary(raw, name):
+            grouped = keep.tile([P, D * PACK], BF16, name=name + "_grouped", align_bytes=64)
+            codes = keep.tile([P, D], U32, name=name + "_codes", align_bytes=64)
+            scales = keep.tile([P, D], U8, name=name + "_scales", align_bytes=64)
+            step = GROUP * PACK
+            for g in range(groups):
+                dst = grouped[:, g * step:(g + 1) * step].rearrange("p (t m j) -> p m j t", t=IN_GROUP, j=PACK)
+                src = raw[:, :, g * GROUP:(g + 1) * GROUP].rearrange("p j (m t) -> p m j t", t=IN_GROUP)
+                if g == 0:
+                    nc.vector.tensor_copy(out=dst, in_=src)
+                else:
+                    nc.scalar.copy(out=dst, in_=src)
+            for g in range(groups):
+                cols = slice(g * GROUP, (g + 1) * GROUP)
+                nc.vector.quantize_mx(
+                    out=codes[:, cols].bitcast(E4M3),
+                    scales=scales[:, cols],
+                    in_=grouped[:, g * step:(g + 1) * step],
+                )
+            return codes, scales
+
+        def moving(raw, fmt, name):
+            grouped = keep.tile([P, T * PACK], BF16, name=name + "_grouped", align_bytes=64)
+            codes = keep.tile([P, T], U32, name=name + "_codes", align_bytes=64)
+            scales = keep.tile([P, T], U8, name=name + "_scales", align_bytes=64)
+            parts = [(0, 256, "v"), (384, 512, "s"), (256, 384, "v")]
+            for c0, c1, engine in parts:
+                dst = grouped[:, c0 * PACK:c1 * PACK].rearrange("p (c i j) -> p c j i", i=4, j=PACK)
+                src = raw[:, :, c0:c1].rearrange("p j (c i) -> p c j i", i=4)
+                if engine == "v":
+                    nc.vector.tensor_copy(out=dst, in_=src)
+                else:
+                    nc.scalar.copy(out=dst, in_=src)
+            for c0, c1 in ((0, 256), (256, 384), (384, 512)):
+                nc.vector.quantize_mx(
+                    out=codes[:, c0:c1].bitcast(fmt),
+                    scales=scales[:, c0:c1],
+                    in_=grouped[:, c0 * PACK:c1 * PACK],
+                )
+            return codes, scales
+
+        acc = [psum.tile([P, T], F32, name="acc%d" % b) for b in range(banks)]
+
+        def run_pass(s, m, m_fmt, first, last):
+            for b in range(banks):
+                cols = slice(b * P, (b + 1) * P)
+                nc.tensor.matmul_mx(
+                    out=acc[b][:],
+                    lhsT=s[0][:, cols].bitcast(E4M3),
+                    lhsT_scale=s[1][:, cols],
+                    rhs=m[0][:].bitcast(m_fmt),
+                    rhs_scale=m[1][:],
+                    start=first,
+                    stop=last,
+                )
+
+        dy_q = moving(dy_raw[0], E5M2, "dy0")
+        w_q = stationary(w_raw[0], "w0")
+        run_pass(w_q, dy_q, E5M2, True, False)
+        dy_q = moving(dy_raw[1], E5M2, "dy1")
+        w_q = stationary(w_raw[1], "w1")
+        run_pass(w_q, dy_q, E5M2, False, False)
+        w_q = stationary(w_raw[2], "w2")
+        v_q = stationary(v_raw, "v")
+        dy_q = moving(dy_raw[2], E5M2, "dy2")
+        run_pass(w_q, dy_q, E5M2, False, False)
+        e_q = moving(e_raw, E4M3, "e")
+        run_pass(v_q, e_q, E4M3, False, True)
+
+        res = keep.tile([P, banks, T], F32, name="res", align_bytes=64)
+        for b in range(banks):
+            nc.vector.tensor_add(out=res[:, b, :], in0=acc[b][:], in1=r_sb[:, b, :])
+            if b % 2 == 1:
+                g, t = divmod(b - 1, IN_GROUP)
+                rows = out[g * GROUP:(g + 1) * GROUP, :].rearrange("(m t) n -> m t n", t=IN_GROUP)
+                nc.sync.dma_start(out=rows[:, t:t + 2, :], in_=res[:, b - 1:b + 1, :])

@@ -44,8 +44,8 @@ def tile_mix_aux_fm_res_kernel(tc, w, dy, v, e, r, out):
         dy_raw[1] = load(dy, 1, "dy1")
         w_raw[1] = load(w, 1, "w1")
         w_raw[2] = load(w, 2, "w2")
-        v_raw = load(v, 0, "v")
         dy_raw[2] = load(dy, 2, "dy2")
+        v_raw = load(v, 0, "v")
         e_raw = load(e, 0, "e")
 
         r_sb = keep.tile([P, banks, T], F32, name="r_sb", align_bytes=64)
@@ -56,46 +56,42 @@ def tile_mix_aux_fm_res_kernel(tc, w, dy, v, e, r, out):
                 in_=rows.rearrange("(m t) n -> m t n", t=IN_GROUP),
             )
 
-        def stationary(raw, name):
-            grouped = keep.tile([P, D * PACK], BF16, name=name + "_grouped", align_bytes=64)
-            codes = keep.tile([P, D], U32, name=name + "_codes", align_bytes=64)
-            scales = keep.tile([P, D], U8, name=name + "_scales", align_bytes=64)
-            step = GROUP * PACK
-            for g in range(groups):
-                dst = grouped[:, g * step:(g + 1) * step].rearrange("p (t m j) -> p m j t", t=IN_GROUP, j=PACK)
-                src = raw[:, :, g * GROUP:(g + 1) * GROUP].rearrange("p j (m t) -> p m j t", t=IN_GROUP)
-                if g == 0:
-                    nc.vector.tensor_copy(out=dst, in_=src)
-                else:
-                    nc.scalar.copy(out=dst, in_=src)
-            for g in range(groups):
-                cols = slice(g * GROUP, (g + 1) * GROUP)
-                nc.vector.quantize_mx(
-                    out=codes[:, cols].bitcast(E4M3),
-                    scales=scales[:, cols],
-                    in_=grouped[:, g * step:(g + 1) * step],
-                )
-            return codes, scales
+        step = GROUP * PACK
 
-        def moving(raw, fmt, name):
-            grouped = keep.tile([P, T * PACK], BF16, name=name + "_grouped", align_bytes=64)
-            codes = keep.tile([P, T], U32, name=name + "_codes", align_bytes=64)
-            scales = keep.tile([P, T], U8, name=name + "_scales", align_bytes=64)
-            parts = [(0, 256, "v"), (384, 512, "s"), (256, 384, "v")]
-            for c0, c1, engine in parts:
-                dst = grouped[:, c0 * PACK:c1 * PACK].rearrange("p (c i j) -> p c j i", i=4, j=PACK)
-                src = raw[:, :, c0:c1].rearrange("p j (c i) -> p c j i", i=4)
-                if engine == "v":
-                    nc.vector.tensor_copy(out=dst, in_=src)
-                else:
-                    nc.scalar.copy(out=dst, in_=src)
-            for c0, c1 in ((0, 256), (256, 384), (384, 512)):
-                nc.vector.quantize_mx(
-                    out=codes[:, c0:c1].bitcast(fmt),
-                    scales=scales[:, c0:c1],
-                    in_=grouped[:, c0 * PACK:c1 * PACK],
+        def alloc(width, name):
+            grouped = keep.tile([P, width * PACK], BF16, name=name + "_grouped", align_bytes=64)
+            codes = keep.tile([P, width], U32, name=name + "_codes", align_bytes=64)
+            scales = keep.tile([P, width], U8, name=name + "_scales", align_bytes=64)
+            return grouped, codes, scales
+
+        def quantize(q, c0, c1, fmt):
+            nc.vector.quantize_mx(
+                out=q[1][:, c0:c1].bitcast(fmt),
+                scales=q[2][:, c0:c1],
+                in_=q[0][:, c0 * PACK:c1 * PACK],
+            )
+
+        def copy_weights(raw, q):
+            for g, copy in ((0, nc.vector.tensor_copy), (1, nc.scalar.copy)):
+                copy(
+                    out=q[0][:, g * step:(g + 1) * step].rearrange("p (t m j) -> p m j t", t=IN_GROUP, j=PACK),
+                    in_=raw[:, :, g * GROUP:(g + 1) * GROUP].rearrange("p j (m t) -> p m j t", t=IN_GROUP),
                 )
-            return codes, scales
+
+        def copy_moving(raw, q):
+            for c0, c1, copy in (
+                (0, 256, nc.vector.tensor_copy),
+                (384, 512, nc.scalar.copy),
+                (256, 384, nc.vector.tensor_copy),
+            ):
+                copy(
+                    out=q[0][:, c0 * PACK:c1 * PACK].rearrange("p (c i j) -> p c j i", i=4, j=PACK),
+                    in_=raw[:, :, c0:c1].rearrange("p j (c i) -> p c j i", i=4),
+                )
+
+        def quantize_moving(q, fmt):
+            for c0, c1 in ((0, 256), (256, 384), (384, 512)):
+                quantize(q, c0, c1, fmt)
 
         acc = [psum.tile([P, T], F32, name="acc%d" % b) for b in range(banks)]
 
@@ -104,31 +100,48 @@ def tile_mix_aux_fm_res_kernel(tc, w, dy, v, e, r, out):
                 cols = slice(b * P, (b + 1) * P)
                 nc.tensor.matmul_mx(
                     out=acc[b][:],
-                    lhsT=s[0][:, cols].bitcast(E4M3),
-                    lhsT_scale=s[1][:, cols],
-                    rhs=m[0][:].bitcast(m_fmt),
-                    rhs_scale=m[1][:],
+                    lhsT=s[1][:, cols].bitcast(E4M3),
+                    lhsT_scale=s[2][:, cols],
+                    rhs=m[1][:].bitcast(m_fmt),
+                    rhs_scale=m[2][:],
                     start=first,
                     stop=last,
                 )
 
-        dy_q = moving(dy_raw[0], E5M2, "dy0")
-        w_q = stationary(w_raw[0], "w0")
-        run_pass(w_q, dy_q, E5M2, True, False)
-        dy_q = moving(dy_raw[1], E5M2, "dy1")
-        w_q = stationary(w_raw[1], "w1")
-        run_pass(w_q, dy_q, E5M2, False, False)
-        w_q = stationary(w_raw[2], "w2")
-        v_q = stationary(v_raw, "v")
-        dy_q = moving(dy_raw[2], E5M2, "dy2")
-        run_pass(w_q, dy_q, E5M2, False, False)
-        e_q = moving(e_raw, E4M3, "e")
+        dy_q = [alloc(T, "dy%d" % c) for c in range(3)]
+        w_q = [alloc(D, "w%d" % c) for c in range(3)]
+        v_q = alloc(D, "v")
+        e_q = alloc(T, "e")
+
+        def do_dy(c):
+            copy_moving(dy_raw[c], dy_q[c])
+            quantize_moving(dy_q[c], E5M2)
+
+        def do_w(c):
+            copy_weights(w_raw[c], w_q[c])
+            quantize(w_q[c], 0, GROUP, E4M3)
+            quantize(w_q[c], GROUP, D, E4M3)
+
+        do_dy(0)
+        do_w(0)
+        run_pass(w_q[0], dy_q[0], E5M2, True, False)
+        do_dy(1)
+        do_w(1)
+        run_pass(w_q[1], dy_q[1], E5M2, False, False)
+        do_w(2)
+        do_dy(2)
+        run_pass(w_q[2], dy_q[2], E5M2, False, False)
+        copy_weights(v_raw, v_q)
+        quantize(v_q, 0, GROUP, E4M3)
+        copy_moving(e_raw, e_q)
+        quantize_moving(e_q, E4M3)
+        quantize(v_q, GROUP, D, E4M3)
         run_pass(v_q, e_q, E4M3, False, True)
 
         res = keep.tile([P, banks, T], F32, name="res", align_bytes=64)
-        for b in range(banks):
-            nc.vector.tensor_add(out=res[:, b, :], in0=acc[b][:], in1=r_sb[:, b, :])
-            if b % 2 == 1:
-                g, t = divmod(b - 1, IN_GROUP)
-                rows = out[g * GROUP:(g + 1) * GROUP, :].rearrange("(m t) n -> m t n", t=IN_GROUP)
-                nc.sync.dma_start(out=rows[:, t:t + 2, :], in_=res[:, b - 1:b + 1, :])
+        for b0, b1 in ((0, 2), (2, 4), (4, 6), (6, 7), (7, 8)):
+            for b in range(b0, b1):
+                nc.vector.tensor_add(out=res[:, b, :], in0=acc[b][:], in1=r_sb[:, b, :])
+            g, t = divmod(b0, IN_GROUP)
+            rows = out[g * GROUP:(g + 1) * GROUP, :].rearrange("(m t) n -> m t n", t=IN_GROUP)
+            nc.sync.dma_start(out=rows[:, t:t + b1 - b0, :], in_=res[:, b0:b1, :])

from contextlib import ExitStack

import concourse.mybir as mybir

K, L, D, T = 1536, 512, 1024, 512

FLOPS = 2 * (K + L) * D * T

F32 = mybir.dt.float32
BF16 = mybir.dt.bfloat16
U32 = mybir.dt.uint32
U8 = mybir.dt.uint8
E4M3 = mybir.dt.float8_e4m3fn_x4
E5M2 = mybir.dt.float8_e5m2_x4

P = 128
PACK = 4
K_PASS = P * PACK
GROUP = 512
IN_GROUP = 4


def tile_mix_aux_fm_res_kernel(tc, w, dy, v, e, r, out):
    nc = tc.nc
    banks = D // P
    groups = D // GROUP

    with ExitStack() as ctx:
        keep = ctx.enter_context(tc.tile_pool(name="keep", bufs=1))
        psum = ctx.enter_context(tc.psum_pool(name="psum", bufs=1))
        ctx.enter_context(tc.manual_schedule())

        def load(src, c, name):
            width = src.shape[1]
            raw = keep.tile([P, PACK, width], F32, name=name + "_raw", align_bytes=64)
            rows = src[c * K_PASS:(c + 1) * K_PASS, :]
            nc.sync.dma_start(out=raw[:], in_=rows.rearrange("(p j) c -> p j c", j=PACK))
            return raw

        dy_raw = {}
        w_raw = {}
        dy_raw[0] = load(dy, 0, "dy0")
        w_raw[0] = load(w, 0, "w0")
        dy_raw[1] = load(dy, 1, "dy1")
        w_raw[1] = load(w, 1, "w1")
        w_raw[2] = load(w, 2, "w2")
        dy_raw[2] = load(dy, 2, "dy2")
        v_raw = load(v, 0, "v")
        e_raw = load(e, 0, "e")

        r_sb = keep.tile([P, banks, T], F32, name="r_sb", align_bytes=64)
        for g in range(groups):
            rows = r[g * GROUP:(g + 1) * GROUP, :]
            nc.sync.dma_start(
                out=r_sb[:, g * IN_GROUP:(g + 1) * IN_GROUP, :],
                in_=rows.rearrange("(m t) n -> m t n", t=IN_GROUP),
            )

        step = GROUP * PACK

        def alloc(width, name):
            grouped = keep.tile([P, width * PACK], BF16, name=name + "_grouped", align_bytes=64)
            codes = keep.tile([P, width], U32, name=name + "_codes", align_bytes=64)
            scales = keep.tile([P, width], U8, name=name + "_scales", align_bytes=64)
            return grouped, codes, scales

        def quantize(q, c0, c1, fmt):
            nc.vector.quantize_mx(
                out=q[1][:, c0:c1].bitcast(fmt),
                scales=q[2][:, c0:c1],
                in_=q[0][:, c0 * PACK:c1 * PACK],
            )

        def copy_weights(raw, q):
            for g, copy in ((0, nc.vector.tensor_copy), (1, nc.scalar.copy)):
                copy(
                    out=q[0][:, g * step:(g + 1) * step].rearrange("p (t m j) -> p m j t", t=IN_GROUP, j=PACK),
                    in_=raw[:, :, g * GROUP:(g + 1) * GROUP].rearrange("p j (m t) -> p m j t", t=IN_GROUP),
                )

        def copy_moving(raw, q):
            for c0, c1, copy in (
                (0, 256, nc.vector.tensor_copy),
                (384, 512, nc.scalar.copy),
                (256, 384, nc.vector.tensor_copy),
            ):
                copy(
                    out=q[0][:, c0 * PACK:c1 * PACK].rearrange("p (c i j) -> p c j i", i=4, j=PACK),
                    in_=raw[:, :, c0:c1].rearrange("p j (c i) -> p c j i", i=4),
                )

        def quantize_moving(q, fmt):
            for c0, c1 in ((0, 256), (256, 384), (384, 512)):
                quantize(q, c0, c1, fmt)

        acc = [psum.tile([P, T], F32, name="acc%d" % b) for b in range(banks)]

        def run_pass(s, m, m_fmt, first, last):
            for b in range(banks):
                cols = slice(b * P, (b + 1) * P)
                nc.tensor.matmul_mx(
                    out=acc[b][:],
                    lhsT=s[1][:, cols].bitcast(E4M3),
                    lhsT_scale=s[2][:, cols],
                    rhs=m[1][:].bitcast(m_fmt),
                    rhs_scale=m[2][:],
                    start=first,
                    stop=last,
                )

        dy_q = [alloc(T, "dy%d" % c) for c in range(3)]
        w_q = [alloc(D, "w%d" % c) for c in range(3)]
        v_q = alloc(D, "v")
        e_q = alloc(T, "e")

        def do_dy(c):
            copy_moving(dy_raw[c], dy_q[c])
            quantize_moving(dy_q[c], E5M2)

        def do_w(c):
            copy_weights(w_raw[c], w_q[c])
            quantize(w_q[c], 0, GROUP, E4M3)
            quantize(w_q[c], GROUP, D, E4M3)

        do_dy(0)
        do_w(0)
        run_pass(w_q[0], dy_q[0], E5M2, True, False)
        do_dy(1)
        do_w(1)
        run_pass(w_q[1], dy_q[1], E5M2, False, False)
        do_w(2)
        do_dy(2)
        run_pass(w_q[2], dy_q[2], E5M2, False, False)
        copy_weights(v_raw, v_q)
        quantize(v_q, 0, GROUP, E4M3)
        copy_moving(e_raw, e_q)
        quantize_moving(e_q, E4M3)
        quantize(v_q, GROUP, D, E4M3)
        run_pass(v_q, e_q, E4M3, False, True)

        res = keep.tile([P, banks, T], F32, name="res", align_bytes=64)
        for b0, b1 in ((0, 2), (2, 4), (4, 6), (6, 7), (7, 8)):
            for b in range(b0, b1):
                nc.vector.tensor_add(out=res[:, b, :], in0=acc[b][:], in1=r_sb[:, b, :])
            g, t = divmod(b0, IN_GROUP)
            rows = out[g * GROUP:(g + 1) * GROUP, :].rearrange("(m t) n -> m t n", t=IN_GROUP)
            nc.sync.dma_start(out=rows[:, t:t + b1 - b0, :], in_=res[:, b0:b1, :])
